import numpy as np
import ml_dtypes


def mxq(x, axis, fmt="e4m3"):
    dtype, down = {"e4m3": (ml_dtypes.float8_e4m3fn, 7), "e5m2": (ml_dtypes.float8_e5m2, 14)}[fmt]
    v = np.moveaxis(np.asarray(x, np.float32).astype(ml_dtypes.bfloat16).astype(np.float64), axis, -1)
    blocks = v.reshape(v.shape[:-1] + (-1, 32))
    amax = np.abs(blocks).max(-1, keepdims=True)
    byte = np.maximum(np.where(amax > 0, np.frexp(amax)[1] - 1 + 127, 0) - down, 1)
    scale = np.exp2(byte - 127.0)
    codes = (blocks / scale).astype(np.float32).astype(dtype).astype(np.float64)
    return np.moveaxis((codes * scale).reshape(v.shape), -1, axis)


WIDE = False


def mx_kscale(k):
    if not WIDE:
        return np.ones(k)
    levels = np.array([10, -10, 5, -5, 0])
    if k % 512:
        return np.exp2(np.random.permutation(np.resize(levels, k // 32))).repeat(32)
    a = np.empty((k // 512, 16))
    for p in range(k // 512):
        a[p, :8] = np.random.permutation(np.resize(levels, 8))
        for g in range(8):
            far = levels[np.abs(levels - a[p, g]) >= 10]
            a[p, g + 8] = far[np.random.randint(len(far))]
    return np.exp2(a.ravel()).repeat(32)


def f64(x):
    return np.asarray(x).astype(np.float64)


def striped(idx):
    return np.tile(np.asarray(idx).reshape(-1, 16).T, (8, 1)).astype(np.uint16)


def unstriped(offs):
    return offs[:16].T.reshape(-1).astype(np.int64)


E2M1 = np.array([0.0, 0.5, 1.0, 1.5, 2.0, 3.0, 4.0, 6.0, -0.0, -0.5, -1.0, -1.5, -2.0, -3.0, -4.0, -6.0])


def pack_weight(w, fmt):
    k, n = w.shape
    w = f64(np.asarray(w, np.float32).astype(ml_dtypes.bfloat16)).reshape(k // 32, 32, n)
    amax = np.abs(w).max(1)
    if fmt == "e4m3":
        byte = np.frexp(amax)[1] - 1 + 127 - 7
    else:
        mant, ex = np.frexp(amax / 6.0)
        byte = np.where(mant > 0.5, ex, ex - 1) + 127
    byte = np.clip(np.where(amax > 0, byte, 1), 1, 254)
    scaled = (w * np.exp2(127.0 - byte)[:, None, :]).reshape(k, n).astype(np.float32)
    by_word = np.ascontiguousarray(scaled.reshape(k // 512, 128, 4, n).transpose(0, 1, 3, 2))
    if fmt == "e4m3":
        words = by_word.astype(ml_dtypes.float8_e4m3fn).view(np.uint8)
    else:
        c = by_word.astype(ml_dtypes.float4_e2m1fn).view(np.uint8) & 0xF
        words = (c[..., 0::2] | (c[..., 1::2] << 4)).reshape(k // 512, 128, 2 * n)
    return np.ascontiguousarray(words), np.ascontiguousarray(byte.astype(np.uint8).reshape(k // 512, 16, n))


def unpack_weight(words, scales, fmt):
    g, _, n = scales.shape
    words = np.ascontiguousarray(words).reshape(g, 128, n, -1)
    if fmt == "e4m3":
        vals = words.view(ml_dtypes.float8_e4m3fn).astype(np.float64)
    else:
        nib = np.empty((g, 128, n, 4), np.uint8)
        nib[..., 0::2] = words & 0xF
        nib[..., 1::2] = words >> 4
        vals = E2M1[nib]
    vals = vals * np.repeat(np.exp2(scales.astype(np.float64) - 127.0), 8, axis=1)[..., None]
    return vals.transpose(0, 1, 3, 2).reshape(g * 512, n)


def silu(v):
    return v / (1.0 + np.exp(-v))


def bf(x):
    return np.asarray(x, np.float32).astype(ml_dtypes.bfloat16)


def planes(Y):
    r, m = Y.shape
    b = f64(bf(Y)).reshape(r // 32, 32, m)
    amax = np.abs(b).max(1)
    byte = np.clip(np.where(amax > 0, np.frexp(amax)[1] - 1 + 127 - 7, 1), 1, 254)
    codes = (b * np.exp2(127.0 - byte)[:, None, :]).reshape(r, m).astype(np.float32).astype(ml_dtypes.float8_e4m3fn).view(np.uint8)
    words = codes.reshape(r // 512, 128, 4, m).transpose(0, 1, 3, 2)
    return np.ascontiguousarray(words), np.ascontiguousarray(byte.astype(np.uint8).reshape(r // 512, 16, m))


K, T, J, B, N = 1024, 1024, 512, 64, 512


def setup_inputs():
    n = np.random.standard_normal
    idx = (np.random.permutation(T // 8)[:J // 8, None] * 8 + np.arange(8)).reshape(-1)
    fk = mx_kscale(K)
    wap = pack_weight(n((K, N)) * 1 / np.sqrt(K) * fk[:, None], "e2m1")
    return {
        "xt": (n((K, T)) / fk[:, None]).astype(np.float32),
        "wa_words": wap[0],
        "wa_scales": wap[1],
        "bw": (np.random.uniform(0.4, 1.4, (N, B))).astype(np.float32),
        "res": (1.0 * n((N, T))).astype(np.float32),
        "offs": striped(idx),
    }


def reference(xt, wa_words, wa_scales, bw, res, offs):
    idx = unstriped(offs)
    wau = unpack_weight(wa_words, wa_scales, "e2m1")
    xtidxq = mxq(f64(xt)[:, idx], 0, "e4m3")
    p = wau.T @ xtidxq
    br = np.repeat(f64(bw), J // B, axis=1)
    d = silu(p * br)
    dp = np.zeros((N, T))
    dp[:, idx] = d
    y = 0.3 * f64(res) + dp
    words, scales = planes(y)
    return y, words, scales

@@ -1,0 +1,175 @@
+from contextlib import ExitStack
+
+import concourse.mybir as mybir
+
+K, T, J, B, N = 1024, 1024, 512, 64, 512
+FLOPS = 2 * K * N * J
+
+F32 = mybir.dt.float32
+BF16 = mybir.dt.bfloat16
+I32 = mybir.dt.int32
+U32 = mybir.dt.uint32
+U16 = mybir.dt.uint16
+U8 = mybir.dt.uint8
+FP8X4 = mybir.dt.float8_e4m3fn_x4
+FP4X4 = mybir.dt.float4_e2m1fn_x4
+ALU = mybir.AluOpType
+ACT = mybir.ActivationFunctionType
+
+P = 128
+PACK = 4
+PASSES = K // (P * PACK)
+RUN = J // B
+HALF = T // 2
+LAST_VECTOR_COLS = 384
+CHUNKS = [128, 256, 256, 256, 128]
+
+
+def tile_moe_block_routed_expert_pl_kernel(tc, xt, wa_words, wa_scales, bw, res, offs, out_0, out_1, out_2):
+    nc = tc.nc
+    x_rows = xt.rearrange("(z p t) c -> z p t c", p=P, t=PACK)
+    res_rows = res.rearrange("(p t) c -> p t c", t=PACK)
+    y_rows = out_0.rearrange("(p t) c -> p t c", t=PACK)
+    code_rows = out_1[0].rearrange("p c r -> p (c r)").bitcast(I32)
+    scale_rows = out_2[0].bitcast(I32)
+
+    with ExitStack() as ctx:
+        keep = ctx.enter_context(tc.tile_pool(name="keep", bufs=1))
+        psum = ctx.enter_context(tc.psum_pool(name="psum", bufs=1))
+
+        offsets = keep.tile([P, J // 16], U16, name="offsets")
+        w_words = keep.tile([P, PASSES, 2 * N], U8, name="w_words", align_bytes=64)
+        w_scales = keep.tile([P, PASSES, N], U8, name="w_scales", align_bytes=64)
+        w_words_dealt = keep.tile([P, PASSES, PACK, 2 * P], U8, name="w_words_dealt", align_bytes=64)
+        w_scales_dealt = keep.tile([P, PASSES, PACK, P], U8, name="w_scales_dealt", align_bytes=64)
+        x_raw = {
+            (z, u, h): keep.tile([P, 2, HALF], F32, name=f"x_raw{z}{u}{h}", align_bytes=64)
+            for z in range(PASSES) for u in range(2) for h in range(2)
+        }
+        dp = [keep.tile([P, T], F32, name=f"dp{t}", align_bytes=64) for t in range(PACK)]
+
+        def load_x(z, u, h):
+            nc.sync.dma_start(out=x_raw[z, u, h][:], in_=x_rows[z, :, 2 * u : 2 * u + 2, h * HALF : (h + 1) * HALF])
+
+        nc.vector.memset(w_scales[:].rearrange("p z c -> p (z c)").bitcast(I32), 0)
+        load_x(0, 0, 0)
+        for q in range(4):
+            nc.sync.dma_start(
+                out=w_scales[32 * q : 32 * q + 4].bitcast(I32),
+                in_=wa_scales[:, 4 * q : 4 * q + 4, :].rearrange("z r c -> r z c").bitcast(I32),
+            )
+        nc.sync.dma_start(out=w_words[:].bitcast(I32), in_=wa_words.rearrange("z p b -> p z b").bitcast(I32))
+        load_x(0, 0, 1)
+        nc.sync.dma_start(offsets[:], offs)
+        for z, u, h in list(x_raw)[2:]:
+            load_x(z, u, h)
+        bw_sb = keep.tile([P, PACK, B], F32, name="bw_sb", align_bytes=64)
+        nc.sync.dma_start(out=bw_sb[:], in_=bw.rearrange("(p t) b -> p t b", t=PACK))
+        res_sb = [keep.tile([P, T], F32, name=f"res{t}", align_bytes=64) for t in range(PACK)]
+        for t in range(PACK):
+            nc.sync.dma_start(out=res_sb[t][:], in_=res_rows[:, t, :])
+
+        for t in range(PACK):
+            nc.vector.memset(dp[t][:], 0.0)
+
+        nc.vector.tensor_copy(
+            out=w_scales_dealt[:], in_=w_scales[:].rearrange("p z (m t) -> p z t m", t=PACK)
+        )
+        nc.vector.tensor_copy(
+            out=w_words_dealt[:].rearrange("p z t (m b) -> p z t m b", b=2),
+            in_=w_words[:].rearrange("p z (m t b) -> p z t m b", t=PACK, b=2),
+        )
+
+        banks = [psum.tile([P, J], F32, name=f"bank{t}") for t in range(PACK)]
+        for z in range(PASSES):
+            picked = keep.tile([P, 2, J], F32, name=f"picked{z}", align_bytes=64)
+            for u in range(2):
+                pairs = keep.tile([P, T], F32, name=f"pairs{z}{u}", align_bytes=64)
+                pairs_bf = pairs[:].bitcast(BF16).rearrange("p (c e) -> p c e", e=2)
+                for h in range(2):
+                    src = x_raw[z, u, h][:].rearrange("p e c -> p c e")
+                    dst = pairs_bf[:, h * HALF : (h + 1) * HALF, :]
+                    cut = LAST_VECTOR_COLS if (z, u, h) == (PASSES - 1, 1, 1) else 0
+                    nc.scalar.activation(dst[:, cut:, :], src[:, cut:, :], ACT.Copy)
+                    if cut:
+                        nc.vector.tensor_copy(out=dst[:, :cut, :], in_=src[:, :cut, :])
+                nc.vector.tensor_copy(out=picked[:, u, :], in_=pairs[:].indirect(offsets[:]))
+            grouped = keep.tile([P, J, 2], I32, name=f"grouped{z}", align_bytes=64)
+            nc.vector.tensor_copy(out=grouped[:], in_=picked[:].bitcast(I32).rearrange("p u j -> p j u"))
+            x_codes = keep.tile([P, J], U32, name=f"x_codes{z}", align_bytes=64)
+            x_scales = keep.tile([P, J], U8, name=f"x_scales{z}", align_bytes=64)
+            nc.vector.quantize_mx(
+                out=x_codes[:].bitcast(FP8X4),
+                scales=x_scales[:],
+                in_=grouped[:].rearrange("p j u -> p (j u)").bitcast(BF16),
+            )
+            for t in range(PACK):
+                nc.tensor.matmul_mx(
+                    out=banks[t][:],
+                    lhsT=w_words_dealt[:, z, t, :].bitcast(FP4X4),
+                    lhsT_scale=w_scales_dealt[:, z, t, :],
+                    rhs=x_codes[:].bitcast(FP8X4),
+                    rhs_scale=x_scales[:],
+                    start=(z == 0),
+                    stop=(z == PASSES - 1),
+                )
+
+        starts = [sum(CHUNKS[:i]) for i in range(len(CHUNKS))]
+        y_bf = [keep.tile([P, w, PACK], BF16, name=f"y_bf{i}", align_bytes=64) for i, w in enumerate(CHUNKS)]
+        y_early = keep.tile([P, 2, T], F32, name="y_early", align_bytes=64)
+        y_late = [keep.tile([P, 2, w], F32, name=f"y_late{i}", align_bytes=64) for i, w in enumerate(CHUNKS)]
+        y_codes = [keep.tile([P, w], U32, name=f"y_codes{i}", align_bytes=64) for i, w in enumerate(CHUNKS)]
+        y_scales = keep.tile([P, T], U8, name="y_scales", align_bytes=64)
+        d = [keep.tile([P, J], F32, name=f"d{t}", align_bytes=64) for t in range(PACK)]
+
+        def gate(t):
+            weighted = keep.tile([P, B, RUN], F32, name=f"weighted{t}", align_bytes=64)
+            nc.vector.tensor_tensor(
+                weighted[:],
+                banks[t][:].rearrange("p (b r) -> p b r", r=RUN),
+                bw_sb[:, t, :].unsqueeze(2).to_broadcast([P, B, RUN]),
+                ALU.mult,
+            )
+            nc.scalar.activation(d[t][:], weighted[:].rearrange("p b r -> p (b r)"), ACT.Silu)
+
+        def scatter(t):
+            nc.vector.tensor_copy(out=dp[t][:].indirect(offsets[:]), in_=d[t][:])
+
+        def add_residual(t, out, cols):
+            nc.vector.scalar_tensor_tensor(out, res_sb[t][:, cols], 0.3, dp[t][:, cols], ALU.mult, ALU.add)
+
+        def quantise(i):
+            cols = slice(starts[i], starts[i] + CHUNKS[i])
+            nc.vector.quantize_mx(
+                out=y_codes[i][:].bitcast(FP8X4),
+                scales=y_scales[:, cols],
+                in_=y_bf[i][:].rearrange("p c t -> p (c t)"),
+            )
+            nc.sync.dma_start(out=code_rows[:, cols], in_=y_codes[i][:].bitcast(I32))
+
+        gate(0)
+        gate(1)
+        scatter(0)
+        gate(2)
+        scatter(1)
+        gate(3)
+        for t in range(2):
+            add_residual(t, y_early[:, t, :], slice(0, T))
+            nc.sync.dma_start(out=y_rows[:, t, :], in_=y_early[:, t, :])
+        for i, w in enumerate(CHUNKS):
+            cols = slice(starts[i], starts[i] + w)
+            nc.scalar.activation(y_bf[i][:, :, 0:2], y_early[:, :, cols].rearrange("p e c -> p c e"), ACT.Copy)
+        scatter(2)
+        scatter(3)
+        for i, w in enumerate(CHUNKS):
+            cols = slice(starts[i], starts[i] + w)
+            for e in range(2):
+                add_residual(2 + e, y_late[i][:, e, :], cols)
+            nc.scalar.activation(y_bf[i][:, :, 2:4], y_late[i][:].rearrange("p e c -> p c e"), ACT.Copy)
+            nc.sync.dma_start(out=y_rows[:, 2:4, cols], in_=y_late[i][:])
+            if i > 0:
+                quantise(i - 1)
+        quantise(len(CHUNKS) - 1)
+        for q in range(4):
+            queue = nc.scalar if q % 2 else nc.sync
+            queue.dma_start(out=scale_rows[4 * q : 4 * q + 4, :], in_=y_scales[32 * q : 32 * q + 4, :].bitcast(I32))

@@ -20,8 +20,9 @@ P = 128
 PACK = 4
 PASSES = K // (P * PACK)
 RUN = J // B
-HALF = T // 2
-LAST_VECTOR_COLS = 384
+LOADS = [(0, 0, 0, T, 640), (0, 1, 0, T, 640), (1, 0, 0, 512, 0), (1, 0, 512, 512, 0), (1, 1, 0, 512, 0), (1, 1, 512, 512, 256)]
+WEAVE_VECTOR = [512, 320]
+CODES_FIRST = 3
 CHUNKS = [128, 256, 256, 256, 128]
 
 
@@ -42,42 +43,39 @@ def tile_moe_block_routed_expert_pl_kernel(tc, xt, wa_words, wa_scales, bw, res,
         w_scales = keep.tile([P, PASSES, N], U8, name="w_scales", align_bytes=64)
         w_words_dealt = keep.tile([P, PASSES, PACK, 2 * P], U8, name="w_words_dealt", align_bytes=64)
         w_scales_dealt = keep.tile([P, PASSES, PACK, P], U8, name="w_scales_dealt", align_bytes=64)
-        x_raw = {
-            (z, u, h): keep.tile([P, 2, HALF], F32, name=f"x_raw{z}{u}{h}", align_bytes=64)
-            for z in range(PASSES) for u in range(2) for h in range(2)
-        }
+        x_raw = [keep.tile([P, 2, ld[3]], F32, name=f"x_raw{i}", align_bytes=64) for i, ld in enumerate(LOADS)]
         dp = [keep.tile([P, T], F32, name=f"dp{t}", align_bytes=64) for t in range(PACK)]
 
-        def load_x(z, u, h):
-            nc.sync.dma_start(out=x_raw[z, u, h][:], in_=x_rows[z, :, 2 * u : 2 * u + 2, h * HALF : (h + 1) * HALF])
+        def load_x(i):
+            z, u, first, width, share = LOADS[i]
+            nc.sync.dma_start(out=x_raw[i][:], in_=x_rows[z, :, 2 * u : 2 * u + 2, first : first + width])
 
         nc.vector.memset(w_scales[:].rearrange("p z c -> p (z c)").bitcast(I32), 0)
-        load_x(0, 0, 0)
+        nc.sync.dma_start(out=w_words[:].bitcast(I32), in_=wa_words.rearrange("z p b -> p z b").bitcast(I32))
+        load_x(0)
         for q in range(4):
             nc.sync.dma_start(
                 out=w_scales[32 * q : 32 * q + 4].bitcast(I32),
                 in_=wa_scales[:, 4 * q : 4 * q + 4, :].rearrange("z r c -> r z c").bitcast(I32),
             )
-        nc.sync.dma_start(out=w_words[:].bitcast(I32), in_=wa_words.rearrange("z p b -> p z b").bitcast(I32))
-        load_x(0, 0, 1)
         nc.sync.dma_start(offsets[:], offs)
-        for z, u, h in list(x_raw)[2:]:
-            load_x(z, u, h)
+        for i in range(1, len(LOADS)):
+            load_x(i)
         bw_sb = keep.tile([P, PACK, B], F32, name="bw_sb", align_bytes=64)
         nc.sync.dma_start(out=bw_sb[:], in_=bw.rearrange("(p t) b -> p t b", t=PACK))
-        res_sb = [keep.tile([P, T], F32, name=f"res{t}", align_bytes=64) for t in range(PACK)]
-        for t in range(PACK):
-            nc.sync.dma_start(out=res_sb[t][:], in_=res_rows[:, t, :])
+        res_sb = [keep.tile([P, 2, T], F32, name=f"res{u}", align_bytes=64) for u in range(2)]
+        for u in range(2):
+            nc.sync.dma_start(out=res_sb[u][:], in_=res_rows[:, 2 * u : 2 * u + 2, :])
 
         for t in range(PACK):
-            nc.vector.memset(dp[t][:], 0.0)
+            (nc.vector if t < 2 else nc.gpsimd).memset(dp[t][:], 0.0)
 
         nc.vector.tensor_copy(
             out=w_scales_dealt[:], in_=w_scales[:].rearrange("p z (m t) -> p z t m", t=PACK)
         )
         nc.vector.tensor_copy(
-            out=w_words_dealt[:].rearrange("p z t (m b) -> p z t m b", b=2),
-            in_=w_words[:].rearrange("p z (m t b) -> p z t m b", t=PACK, b=2),
+            out=w_words_dealt[:].bitcast(U16),
+            in_=w_words[:].bitcast(U16).rearrange("p z (m t) -> p z t m", t=PACK),
         )
 
         banks = [psum.tile([P, J], F32, name=f"bank{t}") for t in range(PACK)]
@@ -86,16 +84,24 @@ def tile_moe_block_routed_expert_pl_kernel(tc, xt, wa_words, wa_scales, bw, res,
             for u in range(2):
                 pairs = keep.tile([P, T], F32, name=f"pairs{z}{u}", align_bytes=64)
                 pairs_bf = pairs[:].bitcast(BF16).rearrange("p (c e) -> p c e", e=2)
-                for h in range(2):
-                    src = x_raw[z, u, h][:].rearrange("p e c -> p c e")
-                    dst = pairs_bf[:, h * HALF : (h + 1) * HALF, :]
-                    cut = LAST_VECTOR_COLS if (z, u, h) == (PASSES - 1, 1, 1) else 0
-                    nc.scalar.activation(dst[:, cut:, :], src[:, cut:, :], ACT.Copy)
-                    if cut:
-                        nc.vector.tensor_copy(out=dst[:, :cut, :], in_=src[:, :cut, :])
+                for i, (lz, lu, first, width, cut) in enumerate(LOADS):
+                    if (lz, lu) == (z, u):
+                        src = x_raw[i][:].rearrange("p e c -> p c e")
+                        dst = pairs_bf[:, first : first + width, :]
+                        if cut < width:
+                            nc.scalar.activation(dst[:, cut:, :], src[:, cut:, :], ACT.Copy)
+                        if cut:
+                            nc.vector.tensor_copy(out=dst[:, :cut, :], in_=src[:, :cut, :])
                 nc.vector.tensor_copy(out=picked[:, u, :], in_=pairs[:].indirect(offsets[:]))
-            grouped = keep.tile([P, J, 2], I32, name=f"grouped{z}", align_bytes=64)
-            nc.vector.tensor_copy(out=grouped[:], in_=picked[:].bitcast(I32).rearrange("p u j -> p j u"))
+            grouped = keep.tile([P, J, 2], U32, name=f"grouped{z}", align_bytes=64)
+            cut = WEAVE_VECTOR[z]
+            if cut < J:
+                nc.scalar.copy(grouped[:, cut:, :], picked[:].bitcast(U32).rearrange("p u j -> p j u")[:, cut:, :])
+            if cut:
+                nc.vector.tensor_copy(
+                    out=grouped[:].bitcast(I32)[:, :cut, :],
+                    in_=picked[:].bitcast(I32).rearrange("p u j -> p j u")[:, :cut, :],
+                )
             x_codes = keep.tile([P, J], U32, name=f"x_codes{z}", align_bytes=64)
             x_scales = keep.tile([P, J], U8, name=f"x_scales{z}", align_bytes=64)
             nc.vector.quantize_mx(
@@ -118,7 +124,7 @@ def tile_moe_block_routed_expert_pl_kernel(tc, xt, wa_words, wa_scales, bw, res,
         y_bf = [keep.tile([P, w, PACK], BF16, name=f"y_bf{i}", align_bytes=64) for i, w in enumerate(CHUNKS)]
         y_early = keep.tile([P, 2, T], F32, name="y_early", align_bytes=64)
         y_late = [keep.tile([P, 2, w], F32, name=f"y_late{i}", align_bytes=64) for i, w in enumerate(CHUNKS)]
-        y_codes = [keep.tile([P, w], U32, name=f"y_codes{i}", align_bytes=64) for i, w in enumerate(CHUNKS)]
+        y_codes = keep.tile([P, T], U32, name="y_codes", align_bytes=64)
         y_scales = keep.tile([P, T], U8, name="y_scales", align_bytes=64)
         d = [keep.tile([P, J], F32, name=f"d{t}", align_bytes=64) for t in range(PACK)]
 
@@ -136,16 +142,18 @@ def tile_moe_block_routed_expert_pl_kernel(tc, xt, wa_words, wa_scales, bw, res,
             nc.vector.tensor_copy(out=dp[t][:].indirect(offsets[:]), in_=d[t][:])
 
         def add_residual(t, out, cols):
-            nc.vector.scalar_tensor_tensor(out, res_sb[t][:, cols], 0.3, dp[t][:, cols], ALU.mult, ALU.add)
+            nc.vector.scalar_tensor_tensor(out, res_sb[t // 2][:, t % 2, cols], 0.3, dp[t][:, cols], ALU.mult, ALU.add)
 
         def quantise(i):
             cols = slice(starts[i], starts[i] + CHUNKS[i])
             nc.vector.quantize_mx(
-                out=y_codes[i][:].bitcast(FP8X4),
+                out=y_codes[:, cols].bitcast(FP8X4),
                 scales=y_scales[:, cols],
                 in_=y_bf[i][:].rearrange("p c t -> p (c t)"),
             )
-            nc.sync.dma_start(out=code_rows[:, cols], in_=y_codes[i][:].bitcast(I32))
+            if i + 1 in (CODES_FIRST, len(CHUNKS)):
+                done = slice(0 if i + 1 == CODES_FIRST else starts[CODES_FIRST], cols.stop)
+                nc.sync.dma_start(out=code_rows[:, done], in_=y_codes[:, done].bitcast(I32))
 
         gate(0)
         gate(1)

@@ -20,9 +20,10 @@ P = 128
 PACK = 4
 PASSES = K // (P * PACK)
 RUN = J // B
-LOADS = [(0, 0, 0, T, 640), (0, 1, 0, T, 640), (1, 0, 0, 512, 0), (1, 0, 512, 512, 0), (1, 1, 0, 512, 0), (1, 1, 512, 512, 256)]
-WEAVE_VECTOR = [512, 320]
-CODES_FIRST = 3
+LOADS = [(0, 0, 0, T, 640), (0, 1, 0, 512, 0), (0, 1, 512, 512, 320), (1, 0, 0, 512, 0), (1, 0, 512, 512, 0), (1, 1, 0, 512, 0), (1, 1, 512, 512, 256)]
+PAIRED = 3
+ROW_STORES = [1, 2, 3, 4]
+CODE_STORES = [1, 2, 4]
 CHUNKS = [128, 256, 256, 256, 128]
 
 
@@ -53,10 +54,10 @@ def tile_moe_block_routed_expert_pl_kernel(tc, xt, wa_words, wa_scales, bw, res,
         nc.vector.memset(w_scales[:].rearrange("p z c -> p (z c)").bitcast(I32), 0)
         nc.sync.dma_start(out=w_words[:].bitcast(I32), in_=wa_words.rearrange("z p b -> p z b").bitcast(I32))
         load_x(0)
-        for q in range(4):
+        for r in range(4):
             nc.sync.dma_start(
-                out=w_scales[32 * q : 32 * q + 4].bitcast(I32),
-                in_=wa_scales[:, 4 * q : 4 * q + 4, :].rearrange("z r c -> r z c").bitcast(I32),
+                out=w_scales[r:P:32].bitcast(I32),
+                in_=wa_scales[:, r:16:4, :].rearrange("z q c -> q z c").bitcast(I32),
             )
         nc.sync.dma_start(offsets[:], offs)
         for i in range(1, len(LOADS)):
@@ -93,15 +94,8 @@ def tile_moe_block_routed_expert_pl_kernel(tc, xt, wa_words, wa_scales, bw, res,
                         if cut:
                             nc.vector.tensor_copy(out=dst[:, :cut, :], in_=src[:, :cut, :])
                 nc.vector.tensor_copy(out=picked[:, u, :], in_=pairs[:].indirect(offsets[:]))
-            grouped = keep.tile([P, J, 2], U32, name=f"grouped{z}", align_bytes=64)
-            cut = WEAVE_VECTOR[z]
-            if cut < J:
-                nc.scalar.copy(grouped[:, cut:, :], picked[:].bitcast(U32).rearrange("p u j -> p j u")[:, cut:, :])
-            if cut:
-                nc.vector.tensor_copy(
-                    out=grouped[:].bitcast(I32)[:, :cut, :],
-                    in_=picked[:].bitcast(I32).rearrange("p u j -> p j u")[:, :cut, :],
-                )
+            grouped = keep.tile([P, J, 2], I32, name=f"grouped{z}", align_bytes=64)
+            nc.vector.tensor_copy(out=grouped[:], in_=picked[:].bitcast(I32).rearrange("p u j -> p j u"))
             x_codes = keep.tile([P, J], U32, name=f"x_codes{z}", align_bytes=64)
             x_scales = keep.tile([P, J], U8, name=f"x_scales{z}", align_bytes=64)
             nc.vector.quantize_mx(
@@ -122,8 +116,7 @@ def tile_moe_block_routed_expert_pl_kernel(tc, xt, wa_words, wa_scales, bw, res,
 
         starts = [sum(CHUNKS[:i]) for i in range(len(CHUNKS))]
         y_bf = [keep.tile([P, w, PACK], BF16, name=f"y_bf{i}", align_bytes=64) for i, w in enumerate(CHUNKS)]
-        y_early = keep.tile([P, 2, T], F32, name="y_early", align_bytes=64)
-        y_late = [keep.tile([P, 2, w], F32, name=f"y_late{i}", align_bytes=64) for i, w in enumerate(CHUNKS)]
+        y = keep.tile([P, PACK, T], F32, name="y", align_bytes=64)
         y_codes = keep.tile([P, T], U32, name="y_codes", align_bytes=64)
         y_scales = keep.tile([P, T], U8, name="y_scales", align_bytes=64)
         d = [keep.tile([P, J], F32, name=f"d{t}", align_bytes=64) for t in range(PACK)]
@@ -141,8 +134,23 @@ def tile_moe_block_routed_expert_pl_kernel(tc, xt, wa_words, wa_scales, bw, res,
         def scatter(t):
             nc.vector.tensor_copy(out=dp[t][:].indirect(offsets[:]), in_=d[t][:])
 
-        def add_residual(t, out, cols):
-            nc.vector.scalar_tensor_tensor(out, res_sb[t // 2][:, t % 2, cols], 0.3, dp[t][:, cols], ALU.mult, ALU.add)
+        def round_rows(i, rows):
+            cols = slice(starts[i], starts[i] + CHUNKS[i])
+            dst = y_bf[i][:, :, rows].rearrange("p (c i) t -> p c t i", i=4)
+            src = y[:, rows, cols].rearrange("p t (c i) -> p c t i", i=4)
+            if i == len(CHUNKS) - 1:
+                nc.vector.tensor_copy(out=dst, in_=src)
+            else:
+                nc.scalar.activation(dst, src, ACT.Copy)
+
+        def since_last(i, marks):
+            before = [m for m in marks if m < i]
+            return slice(starts[before[-1] + 1] if before else 0, starts[i] + CHUNKS[i])
+
+        def add_residual(t, cols):
+            nc.vector.scalar_tensor_tensor(
+                y[:, t, cols], res_sb[t // 2][:, t % 2, cols], 0.3, dp[t][:, cols], ALU.mult, ALU.add
+            )
 
         def quantise(i):
             cols = slice(starts[i], starts[i] + CHUNKS[i])
@@ -151,8 +159,8 @@ def tile_moe_block_routed_expert_pl_kernel(tc, xt, wa_words, wa_scales, bw, res,
                 scales=y_scales[:, cols],
                 in_=y_bf[i][:].rearrange("p c t -> p (c t)"),
             )
-            if i + 1 in (CODES_FIRST, len(CHUNKS)):
-                done = slice(0 if i + 1 == CODES_FIRST else starts[CODES_FIRST], cols.stop)
+            if i in CODE_STORES:
+                done = since_last(i, CODE_STORES)
                 nc.sync.dma_start(out=code_rows[:, done], in_=y_codes[:, done].bitcast(I32))
 
         gate(0)
@@ -162,22 +170,26 @@ def tile_moe_block_routed_expert_pl_kernel(tc, xt, wa_words, wa_scales, bw, res,
         scatter(1)
         gate(3)
         for t in range(2):
-            add_residual(t, y_early[:, t, :], slice(0, T))
-            nc.sync.dma_start(out=y_rows[:, t, :], in_=y_early[:, t, :])
-        for i, w in enumerate(CHUNKS):
-            cols = slice(starts[i], starts[i] + w)
-            nc.scalar.activation(y_bf[i][:, :, 0:2], y_early[:, :, cols].rearrange("p e c -> p c e"), ACT.Copy)
+            add_residual(t, slice(0, T))
+            nc.sync.dma_start(out=y_rows[:, t, :], in_=y[:, t, :])
+        for i in range(PAIRED):
+            round_rows(i, slice(0, 2))
         scatter(2)
         scatter(3)
+        last = len(CHUNKS) - 1
         for i, w in enumerate(CHUNKS):
-            cols = slice(starts[i], starts[i] + w)
-            for e in range(2):
-                add_residual(2 + e, y_late[i][:, e, :], cols)
-            nc.scalar.activation(y_bf[i][:, :, 2:4], y_late[i][:].rearrange("p e c -> p c e"), ACT.Copy)
-            nc.sync.dma_start(out=y_rows[:, 2:4, cols], in_=y_late[i][:])
-            if i > 0:
+            for t in range(2, PACK):
+                add_residual(t, slice(starts[i], starts[i] + w))
+            if i in ROW_STORES:
+                done = since_last(i, ROW_STORES)
+                nc.sync.dma_start(out=y_rows[:, 2:4, done], in_=y[:, 2:4, done])
+            if i == last:
+                quantise(last - 2)
+            round_rows(i, slice(2 if i < PAIRED else 0, PACK))
+            if 0 < i < last - 1:
                 quantise(i - 1)
-        quantise(len(CHUNKS) - 1)
-        for q in range(4):
-            queue = nc.scalar if q % 2 else nc.sync
-            queue.dma_start(out=scale_rows[4 * q : 4 * q + 4, :], in_=y_scales[32 * q : 32 * q + 4, :].bitcast(I32))
+        quantise(last - 1)
+        quantise(last)
+        for r in range(4):
+            queue = nc.scalar if r % 2 else nc.sync
+            queue.dma_start(out=scale_rows[r:16:4, :], in_=y_scales[r:P:32, :].bitcast(I32))

@@ -20,18 +20,31 @@ P = 128
 PACK = 4
 PASSES = K // (P * PACK)
 RUN = J // B
-LOADS = [(0, 0, 0, T, 640), (0, 1, 0, 512, 0), (0, 1, 512, 512, 320), (1, 0, 0, 512, 0), (1, 0, 512, 512, 0), (1, 1, 0, 512, 0), (1, 1, 512, 512, 256)]
+LIST_ROWS = 16
+QUADRANT = 32
+SLOTS = J // 2
+
+X_LOADS = [
+    (0, 0, 0, T, 640),
+    (0, 1, 0, T // 2, 0),
+    (0, 1, T // 2, T // 2, 320),
+    (1, 0, 0, T // 2, 0),
+    (1, 0, T // 2, T // 2, 0),
+    (1, 1, 0, T // 2, 0),
+    (1, 1, T // 2, T // 2, 256),
+]
+
+CHUNKS = [128, 256, 256, 256, 128]
 PAIRED = 3
 ROW_STORES = [1, 2, 3, 4]
 CODE_STORES = [1, 2, 4]
-CHUNKS = [128, 256, 256, 256, 128]
 
 
 def tile_moe_block_routed_expert_pl_kernel(tc, xt, wa_words, wa_scales, bw, res, offs, out_0, out_1, out_2):
     nc = tc.nc
-    x_rows = xt.rearrange("(z p t) c -> z p t c", p=P, t=PACK)
-    res_rows = res.rearrange("(p t) c -> p t c", t=PACK)
-    y_rows = out_0.rearrange("(p t) c -> p t c", t=PACK)
+    x_rows = xt.rearrange("(z p r) c -> z p r c", p=P, r=PACK)
+    res_rows = res.rearrange("(p r) c -> p r c", r=PACK)
+    y_rows = out_0.rearrange("(p r) c -> p r c", r=PACK)
     code_rows = out_1[0].rearrange("p c r -> p (c r)").bitcast(I32)
     scale_rows = out_2[0].bitcast(I32)
 
@@ -39,75 +52,78 @@ def tile_moe_block_routed_expert_pl_kernel(tc, xt, wa_words, wa_scales, bw, res,
         keep = ctx.enter_context(tc.tile_pool(name="keep", bufs=1))
         psum = ctx.enter_context(tc.psum_pool(name="psum", bufs=1))
 
-        offsets = keep.tile([P, J // 16], U16, name="offsets")
+        offsets = keep.tile([P, J // LIST_ROWS], U16, name="offsets")
         w_words = keep.tile([P, PASSES, 2 * N], U8, name="w_words", align_bytes=64)
         w_scales = keep.tile([P, PASSES, N], U8, name="w_scales", align_bytes=64)
         w_words_dealt = keep.tile([P, PASSES, PACK, 2 * P], U8, name="w_words_dealt", align_bytes=64)
         w_scales_dealt = keep.tile([P, PASSES, PACK, P], U8, name="w_scales_dealt", align_bytes=64)
-        x_raw = [keep.tile([P, 2, ld[3]], F32, name=f"x_raw{i}", align_bytes=64) for i, ld in enumerate(LOADS)]
-        dp = [keep.tile([P, T], F32, name=f"dp{t}", align_bytes=64) for t in range(PACK)]
+        x_raw = [keep.tile([P, 2, load[3]], F32, name=f"x_raw{i}", align_bytes=64) for i, load in enumerate(X_LOADS)]
+        dp = [keep.tile([P, T], F32, name=f"dp{r}", align_bytes=64) for r in range(PACK)]
 
         def load_x(i):
-            z, u, first, width, share = LOADS[i]
+            z, u, first, width = X_LOADS[i][:4]
             nc.sync.dma_start(out=x_raw[i][:], in_=x_rows[z, :, 2 * u : 2 * u + 2, first : first + width])
 
         nc.vector.memset(w_scales[:].rearrange("p z c -> p (z c)").bitcast(I32), 0)
         nc.sync.dma_start(out=w_words[:].bitcast(I32), in_=wa_words.rearrange("z p b -> p z b").bitcast(I32))
         load_x(0)
-        for r in range(4):
+        for i in range(4):
             nc.sync.dma_start(
-                out=w_scales[r:P:32].bitcast(I32),
-                in_=wa_scales[:, r:16:4, :].rearrange("z q c -> q z c").bitcast(I32),
+                out=w_scales[i:P:QUADRANT].bitcast(I32),
+                in_=wa_scales[:, i:16:4, :].rearrange("z q c -> q z c").bitcast(I32),
             )
         nc.sync.dma_start(offsets[:], offs)
-        for i in range(1, len(LOADS)):
+        for i in range(1, len(X_LOADS)):
             load_x(i)
         bw_sb = keep.tile([P, PACK, B], F32, name="bw_sb", align_bytes=64)
-        nc.sync.dma_start(out=bw_sb[:], in_=bw.rearrange("(p t) b -> p t b", t=PACK))
+        nc.sync.dma_start(out=bw_sb[:], in_=bw.rearrange("(p r) b -> p r b", r=PACK))
         res_sb = [keep.tile([P, 2, T], F32, name=f"res{u}", align_bytes=64) for u in range(2)]
         for u in range(2):
             nc.sync.dma_start(out=res_sb[u][:], in_=res_rows[:, 2 * u : 2 * u + 2, :])
 
-        for t in range(PACK):
-            (nc.vector if t < 2 else nc.gpsimd).memset(dp[t][:], 0.0)
+        for r in range(PACK):
+            (nc.vector if r < 2 else nc.gpsimd).memset(dp[r][:], 0.0)
 
         nc.vector.tensor_copy(
-            out=w_scales_dealt[:], in_=w_scales[:].rearrange("p z (m t) -> p z t m", t=PACK)
+            out=w_scales_dealt[:], in_=w_scales[:].rearrange("p z (m r) -> p z r m", r=PACK)
         )
         nc.vector.tensor_copy(
             out=w_words_dealt[:].bitcast(U16),
-            in_=w_words[:].bitcast(U16).rearrange("p z (m t) -> p z t m", t=PACK),
+            in_=w_words[:].bitcast(U16).rearrange("p z (m r) -> p z r m", r=PACK),
         )
 
-        banks = [psum.tile([P, J], F32, name=f"bank{t}") for t in range(PACK)]
+        banks = [psum.tile([P, J], F32, name=f"bank{r}") for r in range(PACK)]
         for z in range(PASSES):
-            picked = keep.tile([P, 2, J], F32, name=f"picked{z}", align_bytes=64)
+            picked = [keep.tile([P, 2, SLOTS], F32, name=f"picked{z}{s}", align_bytes=64) for s in range(2)]
             for u in range(2):
                 pairs = keep.tile([P, T], F32, name=f"pairs{z}{u}", align_bytes=64)
                 pairs_bf = pairs[:].bitcast(BF16).rearrange("p (c e) -> p c e", e=2)
-                for i, (lz, lu, first, width, cut) in enumerate(LOADS):
-                    if (lz, lu) == (z, u):
+                for i, (load_z, load_u, first, width, cut) in enumerate(X_LOADS):
+                    if (load_z, load_u) == (z, u):
                         src = x_raw[i][:].rearrange("p e c -> p c e")
                         dst = pairs_bf[:, first : first + width, :]
-                        if cut < width:
-                            nc.scalar.activation(dst[:, cut:, :], src[:, cut:, :], ACT.Copy)
+                        nc.scalar.activation(dst[:, cut:, :], src[:, cut:, :], ACT.Copy)
                         if cut:
                             nc.vector.tensor_copy(out=dst[:, :cut, :], in_=src[:, :cut, :])
-                nc.vector.tensor_copy(out=picked[:, u, :], in_=pairs[:].indirect(offsets[:]))
-            grouped = keep.tile([P, J, 2], I32, name=f"grouped{z}", align_bytes=64)
-            nc.vector.tensor_copy(out=grouped[:], in_=picked[:].bitcast(I32).rearrange("p u j -> p j u"))
+                for s in range(2):
+                    part = offsets[:, s * SLOTS // LIST_ROWS : (s + 1) * SLOTS // LIST_ROWS]
+                    nc.vector.tensor_copy(out=picked[s][:, u, :], in_=pairs[:].indirect(part))
+            grouped = [keep.tile([P, SLOTS, 2], I32, name=f"grouped{z}{s}", align_bytes=64) for s in range(2)]
+            for s in range(2):
+                nc.vector.tensor_copy(out=grouped[s][:], in_=picked[s][:].bitcast(I32).rearrange("p u j -> p j u"))
             x_codes = keep.tile([P, J], U32, name=f"x_codes{z}", align_bytes=64)
             x_scales = keep.tile([P, J], U8, name=f"x_scales{z}", align_bytes=64)
-            nc.vector.quantize_mx(
-                out=x_codes[:].bitcast(FP8X4),
-                scales=x_scales[:],
-                in_=grouped[:].rearrange("p j u -> p (j u)").bitcast(BF16),
-            )
-            for t in range(PACK):
+            for s in range(2):
+                nc.vector.quantize_mx(
+                    out=x_codes[:, s * SLOTS : (s + 1) * SLOTS].bitcast(FP8X4),
+                    scales=x_scales[:, s * SLOTS : (s + 1) * SLOTS],
+                    in_=grouped[s][:].rearrange("p j u -> p (j u)").bitcast(BF16),
+                )
+            for r in range(PACK):
                 nc.tensor.matmul_mx(
-                    out=banks[t][:],
-                    lhsT=w_words_dealt[:, z, t, :].bitcast(FP4X4),
-                    lhsT_scale=w_scales_dealt[:, z, t, :],
+                    out=banks[r][:],
+                    lhsT=w_words_dealt[:, z, r, :].bitcast(FP4X4),
+                    lhsT_scale=w_scales_dealt[:, z, r, :],
                     rhs=x_codes[:].bitcast(FP8X4),
                     rhs_scale=x_scales[:],
                     start=(z == 0),
@@ -115,73 +131,75 @@ def tile_moe_block_routed_expert_pl_kernel(tc, xt, wa_words, wa_scales, bw, res,
                 )
 
         starts = [sum(CHUNKS[:i]) for i in range(len(CHUNKS))]
+        last = len(CHUNKS) - 1
         y_bf = [keep.tile([P, w, PACK], BF16, name=f"y_bf{i}", align_bytes=64) for i, w in enumerate(CHUNKS)]
         y = keep.tile([P, PACK, T], F32, name="y", align_bytes=64)
         y_codes = keep.tile([P, T], U32, name="y_codes", align_bytes=64)
         y_scales = keep.tile([P, T], U8, name="y_scales", align_bytes=64)
-        d = [keep.tile([P, J], F32, name=f"d{t}", align_bytes=64) for t in range(PACK)]
+        d = [keep.tile([P, J], F32, name=f"d{r}", align_bytes=64) for r in range(PACK)]
 
-        def gate(t):
-            weighted = keep.tile([P, B, RUN], F32, name=f"weighted{t}", align_bytes=64)
+        def chunk(i):
+            return slice(starts[i], starts[i] + CHUNKS[i])
+
+        def since_last_store(i, stores):
+            before = [s for s in stores if s < i]
+            return slice(starts[before[-1] + 1] if before else 0, chunk(i).stop)
+
+        def activate(r):
+            weighted = keep.tile([P, B, RUN], F32, name=f"weighted{r}", align_bytes=64)
             nc.vector.tensor_tensor(
                 weighted[:],
-                banks[t][:].rearrange("p (b r) -> p b r", r=RUN),
-                bw_sb[:, t, :].unsqueeze(2).to_broadcast([P, B, RUN]),
+                banks[r][:].rearrange("p (b i) -> p b i", i=RUN),
+                bw_sb[:, r, :].unsqueeze(2).to_broadcast([P, B, RUN]),
                 ALU.mult,
             )
-            nc.scalar.activation(d[t][:], weighted[:].rearrange("p b r -> p (b r)"), ACT.Silu)
+            nc.scalar.activation(d[r][:], weighted[:].rearrange("p b i -> p (b i)"), ACT.Silu)
 
-        def scatter(t):
-            nc.vector.tensor_copy(out=dp[t][:].indirect(offsets[:]), in_=d[t][:])
+        def scatter(r):
+            nc.vector.tensor_copy(out=dp[r][:].indirect(offsets[:]), in_=d[r][:])
+
+        def add_residual(r, cols):
+            nc.vector.scalar_tensor_tensor(
+                y[:, r, cols], res_sb[r // 2][:, r % 2, cols], 0.3, dp[r][:, cols], ALU.mult, ALU.add
+            )
 
         def round_rows(i, rows):
-            cols = slice(starts[i], starts[i] + CHUNKS[i])
-            dst = y_bf[i][:, :, rows].rearrange("p (c i) t -> p c t i", i=4)
-            src = y[:, rows, cols].rearrange("p t (c i) -> p c t i", i=4)
-            if i == len(CHUNKS) - 1:
+            dst = y_bf[i][:, :, rows].rearrange("p (c i) r -> p c r i", i=4)
+            src = y[:, rows, chunk(i)].rearrange("p r (c i) -> p c r i", i=4)
+            if i == last:
                 nc.vector.tensor_copy(out=dst, in_=src)
             else:
                 nc.scalar.activation(dst, src, ACT.Copy)
 
-        def since_last(i, marks):
-            before = [m for m in marks if m < i]
-            return slice(starts[before[-1] + 1] if before else 0, starts[i] + CHUNKS[i])
-
-        def add_residual(t, cols):
-            nc.vector.scalar_tensor_tensor(
-                y[:, t, cols], res_sb[t // 2][:, t % 2, cols], 0.3, dp[t][:, cols], ALU.mult, ALU.add
-            )
-
         def quantise(i):
-            cols = slice(starts[i], starts[i] + CHUNKS[i])
             nc.vector.quantize_mx(
-                out=y_codes[:, cols].bitcast(FP8X4),
-                scales=y_scales[:, cols],
-                in_=y_bf[i][:].rearrange("p c t -> p (c t)"),
+                out=y_codes[:, chunk(i)].bitcast(FP8X4),
+                scales=y_scales[:, chunk(i)],
+                in_=y_bf[i][:].rearrange("p c r -> p (c r)"),
             )
             if i in CODE_STORES:
-                done = since_last(i, CODE_STORES)
+                done = since_last_store(i, CODE_STORES)
                 nc.sync.dma_start(out=code_rows[:, done], in_=y_codes[:, done].bitcast(I32))
 
-        gate(0)
-        gate(1)
+        activate(0)
+        activate(1)
         scatter(0)
-        gate(2)
+        activate(2)
         scatter(1)
-        gate(3)
-        for t in range(2):
-            add_residual(t, slice(0, T))
-            nc.sync.dma_start(out=y_rows[:, t, :], in_=y[:, t, :])
+        activate(3)
+        for r in range(2):
+            add_residual(r, slice(0, T))
+            nc.sync.dma_start(out=y_rows[:, r, :], in_=y[:, r, :])
         for i in range(PAIRED):
             round_rows(i, slice(0, 2))
         scatter(2)
         scatter(3)
-        last = len(CHUNKS) - 1
-        for i, w in enumerate(CHUNKS):
-            for t in range(2, PACK):
-                add_residual(t, slice(starts[i], starts[i] + w))
+
+        for i in range(len(CHUNKS)):
+            for r in range(2, PACK):
+                add_residual(r, chunk(i))
             if i in ROW_STORES:
-                done = since_last(i, ROW_STORES)
+                done = since_last_store(i, ROW_STORES)
                 nc.sync.dma_start(out=y_rows[:, 2:4, done], in_=y[:, 2:4, done])
             if i == last:
                 quantise(last - 2)
@@ -190,6 +208,7 @@ def tile_moe_block_routed_expert_pl_kernel(tc, xt, wa_words, wa_scales, bw, res,
                 quantise(i - 1)
         quantise(last - 1)
         quantise(last)
-        for r in range(4):
-            queue = nc.scalar if r % 2 else nc.sync
-            queue.dma_start(out=scale_rows[r:16:4, :], in_=y_scales[r:P:32, :].bitcast(I32))
+
+        for i in range(4):
+            queue = nc.scalar if i % 2 else nc.sync
+            queue.dma_start(out=scale_rows[i:16:4, :], in_=y_scales[i:P:QUADRANT, :].bitcast(I32))

from contextlib import ExitStack

import concourse.mybir as mybir

K, T, J, B, N = 1024, 1024, 512, 64, 512
FLOPS = 2 * K * N * J

F32 = mybir.dt.float32
BF16 = mybir.dt.bfloat16
I32 = mybir.dt.int32
U32 = mybir.dt.uint32
U16 = mybir.dt.uint16
U8 = mybir.dt.uint8
FP8X4 = mybir.dt.float8_e4m3fn_x4
FP4X4 = mybir.dt.float4_e2m1fn_x4
ALU = mybir.AluOpType
ACT = mybir.ActivationFunctionType

P = 128
PACK = 4
PASSES = K // (P * PACK)
RUN = J // B
LIST_ROWS = 16
QUADRANT = 32
SLOTS = J // 2

X_LOADS = [
    (0, 0, 0, T, 640),
    (0, 1, 0, T // 2, 0),
    (0, 1, T // 2, T // 2, 320),
    (1, 0, 0, T // 2, 0),
    (1, 0, T // 2, T // 2, 0),
    (1, 1, 0, T // 2, 0),
    (1, 1, T // 2, T // 2, 256),
]

CHUNKS = [128, 256, 256, 256, 128]
PAIRED = 3
ROW_STORES = [1, 2, 3, 4]
CODE_STORES = [1, 2, 4]


def tile_moe_block_routed_expert_pl_kernel(tc, xt, wa_words, wa_scales, bw, res, offs, out_0, out_1, out_2):
    nc = tc.nc
    x_rows = xt.rearrange("(z p r) c -> z p r c", p=P, r=PACK)
    res_rows = res.rearrange("(p r) c -> p r c", r=PACK)
    y_rows = out_0.rearrange("(p r) c -> p r c", r=PACK)
    code_rows = out_1[0].rearrange("p c r -> p (c r)").bitcast(I32)
    scale_rows = out_2[0].bitcast(I32)

    with ExitStack() as ctx:
        keep = ctx.enter_context(tc.tile_pool(name="keep", bufs=1))
        psum = ctx.enter_context(tc.psum_pool(name="psum", bufs=1))

        offsets = keep.tile([P, J // LIST_ROWS], U16, name="offsets")
        w_words = keep.tile([P, PASSES, 2 * N], U8, name="w_words", align_bytes=64)
        w_scales = keep.tile([P, PASSES, N], U8, name="w_scales", align_bytes=64)
        w_words_dealt = keep.tile([P, PASSES, PACK, 2 * P], U8, name="w_words_dealt", align_bytes=64)
        w_scales_dealt = keep.tile([P, PASSES, PACK, P], U8, name="w_scales_dealt", align_bytes=64)
        x_raw = [keep.tile([P, 2, load[3]], F32, name=f"x_raw{i}", align_bytes=64) for i, load in enumerate(X_LOADS)]
        dp = [keep.tile([P, T], F32, name=f"dp{r}", align_bytes=64) for r in range(PACK)]

        def load_x(i):
            z, u, first, width = X_LOADS[i][:4]
            nc.sync.dma_start(out=x_raw[i][:], in_=x_rows[z, :, 2 * u : 2 * u + 2, first : first + width])

        nc.vector.memset(w_scales[:].rearrange("p z c -> p (z c)").bitcast(I32), 0)
        nc.sync.dma_start(out=w_words[:].bitcast(I32), in_=wa_words.rearrange("z p b -> p z b").bitcast(I32))
        load_x(0)
        for i in range(4):
            nc.sync.dma_start(
                out=w_scales[i:P:QUADRANT].bitcast(I32),
                in_=wa_scales[:, i:16:4, :].rearrange("z q c -> q z c").bitcast(I32),
            )
        nc.sync.dma_start(offsets[:], offs)
        for i in range(1, len(X_LOADS)):
            load_x(i)
        bw_sb = keep.tile([P, PACK, B], F32, name="bw_sb", align_bytes=64)
        nc.sync.dma_start(out=bw_sb[:], in_=bw.rearrange("(p r) b -> p r b", r=PACK))
        res_sb = [keep.tile([P, 2, T], F32, name=f"res{u}", align_bytes=64) for u in range(2)]
        for u in range(2):
            nc.sync.dma_start(out=res_sb[u][:], in_=res_rows[:, 2 * u : 2 * u + 2, :])

        for r in range(PACK):
            (nc.vector if r < 2 else nc.gpsimd).memset(dp[r][:], 0.0)

        nc.vector.tensor_copy(
            out=w_scales_dealt[:], in_=w_scales[:].rearrange("p z (m r) -> p z r m", r=PACK)
        )
        nc.vector.tensor_copy(
            out=w_words_dealt[:].bitcast(U16),
            in_=w_words[:].bitcast(U16).rearrange("p z (m r) -> p z r m", r=PACK),
        )

        banks = [psum.tile([P, J], F32, name=f"bank{r}") for r in range(PACK)]
        for z in range(PASSES):
            picked = [keep.tile([P, 2, SLOTS], F32, name=f"picked{z}{s}", align_bytes=64) for s in range(2)]
            for u in range(2):
                pairs = keep.tile([P, T], F32, name=f"pairs{z}{u}", align_bytes=64)
                pairs_bf = pairs[:].bitcast(BF16).rearrange("p (c e) -> p c e", e=2)
                for i, (load_z, load_u, first, width, cut) in enumerate(X_LOADS):
                    if (load_z, load_u) == (z, u):
                        src = x_raw[i][:].rearrange("p e c -> p c e")
                        dst = pairs_bf[:, first : first + width, :]
                        nc.scalar.activation(dst[:, cut:, :], src[:, cut:, :], ACT.Copy)
                        if cut:
                            nc.vector.tensor_copy(out=dst[:, :cut, :], in_=src[:, :cut, :])
                for s in range(2):
                    part = offsets[:, s * SLOTS // LIST_ROWS : (s + 1) * SLOTS // LIST_ROWS]
                    nc.vector.tensor_copy(out=picked[s][:, u, :], in_=pairs[:].indirect(part))
            grouped = [keep.tile([P, SLOTS, 2], I32, name=f"grouped{z}{s}", align_bytes=64) for s in range(2)]
            for s in range(2):
                nc.vector.tensor_copy(out=grouped[s][:], in_=picked[s][:].bitcast(I32).rearrange("p u j -> p j u"))
            x_codes = keep.tile([P, J], U32, name=f"x_codes{z}", align_bytes=64)
            x_scales = keep.tile([P, J], U8, name=f"x_scales{z}", align_bytes=64)
            for s in range(2):
                nc.vector.quantize_mx(
                    out=x_codes[:, s * SLOTS : (s + 1) * SLOTS].bitcast(FP8X4),
                    scales=x_scales[:, s * SLOTS : (s + 1) * SLOTS],
                    in_=grouped[s][:].rearrange("p j u -> p (j u)").bitcast(BF16),
                )
            for r in range(PACK):
                nc.tensor.matmul_mx(
                    out=banks[r][:],
                    lhsT=w_words_dealt[:, z, r, :].bitcast(FP4X4),
                    lhsT_scale=w_scales_dealt[:, z, r, :],
                    rhs=x_codes[:].bitcast(FP8X4),
                    rhs_scale=x_scales[:],
                    start=(z == 0),
                    stop=(z == PASSES - 1),
                )

        starts = [sum(CHUNKS[:i]) for i in range(len(CHUNKS))]
        last = len(CHUNKS) - 1
        y_bf = [keep.tile([P, w, PACK], BF16, name=f"y_bf{i}", align_bytes=64) for i, w in enumerate(CHUNKS)]
        y = keep.tile([P, PACK, T], F32, name="y", align_bytes=64)
        y_codes = keep.tile([P, T], U32, name="y_codes", align_bytes=64)
        y_scales = keep.tile([P, T], U8, name="y_scales", align_bytes=64)
        d = [keep.tile([P, J], F32, name=f"d{r}", align_bytes=64) for r in range(PACK)]

        def chunk(i):
            return slice(starts[i], starts[i] + CHUNKS[i])

        def since_last_store(i, stores):
            before = [s for s in stores if s < i]
            return slice(starts[before[-1] + 1] if before else 0, chunk(i).stop)

        def activate(r):
            weighted = keep.tile([P, B, RUN], F32, name=f"weighted{r}", align_bytes=64)
            nc.vector.tensor_tensor(
                weighted[:],
                banks[r][:].rearrange("p (b i) -> p b i", i=RUN),
                bw_sb[:, r, :].unsqueeze(2).to_broadcast([P, B, RUN]),
                ALU.mult,
            )
            nc.scalar.activation(d[r][:], weighted[:].rearrange("p b i -> p (b i)"), ACT.Silu)

        def scatter(r):
            nc.vector.tensor_copy(out=dp[r][:].indirect(offsets[:]), in_=d[r][:])

        def add_residual(r, cols):
            nc.vector.scalar_tensor_tensor(
                y[:, r, cols], res_sb[r // 2][:, r % 2, cols], 0.3, dp[r][:, cols], ALU.mult, ALU.add
            )

        def round_rows(i, rows):
            dst = y_bf[i][:, :, rows].rearrange("p (c i) r -> p c r i", i=4)
            src = y[:, rows, chunk(i)].rearrange("p r (c i) -> p c r i", i=4)
            if i == last:
                nc.vector.tensor_copy(out=dst, in_=src)
            else:
                nc.scalar.activation(dst, src, ACT.Copy)

        def quantise(i):
            nc.vector.quantize_mx(
                out=y_codes[:, chunk(i)].bitcast(FP8X4),
                scales=y_scales[:, chunk(i)],
                in_=y_bf[i][:].rearrange("p c r -> p (c r)"),
            )
            if i in CODE_STORES:
                done = since_last_store(i, CODE_STORES)
                nc.sync.dma_start(out=code_rows[:, done], in_=y_codes[:, done].bitcast(I32))

        activate(0)
        activate(1)
        scatter(0)
        activate(2)
        scatter(1)
        activate(3)
        for r in range(2):
            add_residual(r, slice(0, T))
            nc.sync.dma_start(out=y_rows[:, r, :], in_=y[:, r, :])
        for i in range(PAIRED):
            round_rows(i, slice(0, 2))
        scatter(2)
        scatter(3)

        for i in range(len(CHUNKS)):
            for r in range(2, PACK):
                add_residual(r, chunk(i))
            if i in ROW_STORES:
                done = since_last_store(i, ROW_STORES)
                nc.sync.dma_start(out=y_rows[:, 2:4, done], in_=y[:, 2:4, done])
            if i == last:
                quantise(last - 2)
            round_rows(i, slice(2 if i < PAIRED else 0, PACK))
            if 0 < i < last - 1:
                quantise(i - 1)
        quantise(last - 1)
        quantise(last)

        for i in range(4):
            queue = nc.scalar if i % 2 else nc.sync
            queue.dma_start(out=scale_rows[i:16:4, :], in_=y_scales[i:P:QUADRANT, :].bitcast(I32))
